import numpy as np, ml_dtypes
CORES = [1,14,19,24,37,42,55,60,65,78,83,88,101,106,119,124]
N = 16
TK, LAY = 64, 4
def setup_inputs(rng):
    return {"x": rng.standard_normal((N, 128, TK), dtype=np.float32).astype(ml_dtypes.bfloat16), "w": (rng.standard_normal((N, 128, LAY * 256), dtype=np.float32) / 16).astype(ml_dtypes.bfloat16)}
def setup_inputs_big(rng):
    d = setup_inputs(rng)
    for k in ("x",): d[k] = (d[k].astype(np.float32) * 1048576.0).astype(d[k].dtype)
    return d
def setup_inputs_small(rng):
    d = setup_inputs(rng)
    for k in ("x",): d[k] = (d[k].astype(np.float32) * (1 / 1048576.0)).astype(d[k].dtype)
    return d
def setup_inputs_apart(rng):
    d = setup_inputs(rng)
    f = (10.0 ** rng.permutation(np.linspace(-1.5, 1.5, N))).astype(np.float32).reshape(N, 1, 1)
    for k in ("x",): d[k] = (d[k].astype(np.float32) * f).astype(d[k].dtype)
    return d
def reference(x, w):
    X, W = x.astype(np.float64), w.astype(np.float64)
    h = list(X)
    for l in range(LAY):
        h = [np.maximum(W[r][:, 256 * l:256 * l + 128].T @ h[r] + W[r][:, 256 * l + 128:256 * l + 256].T @ h[r ^ (1 << l)], 0.0) for r in range(N)]
    return {"y": np.stack(h).astype(ml_dtypes.bfloat16)}

from concourse.bass import DstId, RemoteDMATransfer
from concourse.mybir import AluOpType

TK = 64

SCRATCH = {}
for _n in ("xs", "xa", "xb", "xr", "xrel", "h1", "h1b", "h2", "h2a", "h2b", "h2c", "h3", "h3b", "yb"):
    SCRATCH[_n] = ("sbuf", [128, TK], "bfloat16")
for _n in ("w0", "w1", "w2", "w3", "w0b", "w2b"):
    SCRATCH[_n] = ("sbuf", [128, 256], "bfloat16")
SCRATCH["zero"] = ("sbuf", [128, TK], "float32")
for _n in ("p0", "p0b", "p1", "p2", "p2b", "p3"):
    SCRATCH[_n] = ("psum", [128, 512], "float32")

SEMAPHORES = ["ld_x", "ld_w0", "ld_w1", "ld_w2", "ld_w3", "st", "zs", "sent",
              "a_xa", "a_xb", "a_xr", "a_xrel", "a_w0", "a_h1", "a_w2", "a_h2",
              "mm0", "mm0b", "mm1", "mm2", "mm2b", "mm3",
              "act0", "act0b", "act1", "act2", "act2b", "act3"]


def _plan(cores, topo):
    n = len(cores)

    def ok(a, b):
        return topo.may_write(cores[a], cores[b])

    direct = [ok(r ^ 1, r) for r in range(n)]
    raw = {}
    for s in range(n):
        if direct[s ^ 1]:
            raw[(s, "xa")] = ("xs", [(s ^ 1, "xa")], "a_xa")
        else:
            q = [s ^ d for d in range(2, n) if ok(s, s ^ d) and ok(s ^ d, s ^ 1) and ok(s ^ d, s ^ 3)][0]
            assert (q, "rel") not in raw
            raw[(s, "xr")] = ("xs", [(q, "xr")], "a_xr")
            raw[(q, "rel")] = ("xr", [(s ^ 1, "xrel"), (s ^ 3, "xrel")], "a_xrel")
        if direct[s]:
            raw[(s, "h1")] = ("h1", [(s ^ 2, "h1b")], "a_h1")
        else:
            assert direct[s ^ 2]
            raw[(s, "xb")] = ("xs", [(s ^ 2, "xb")], "a_xb")
            raw[(s, "w0")] = ("w0", [(s ^ 2, "w0b")], "a_w0")
        raw[(s, "w2")] = ("w2", [(s ^ 8, "w2b")], "a_w2")
        raw[(s, "h2")] = ("h2", [(s ^ 4, "h2a"), (s ^ 8, "h2b"), (s ^ 12, "h2c")], "a_h2")
    sends = {}
    expect = [dict() for _ in range(n)]
    for (s, tag), (src, dests, sem) in raw.items():
        mask = -1
        for d, _b in dests:
            assert ok(s, d)
            mask &= topo.mask(cores[s], cores[d])
        sends[(s, tag)] = (src, dests, sem, mask)
        for d, _b in dests:
            expect[d][sem] = expect[d].get(sem, 0) + bin(mask).count("1")
    return direct, sends, expect


def rank_program(g, core, T, topo):
    r = T.rank_of(core)
    if r is None:
        return
    cores = list(T.cores)
    direct, sends, expect = _plan(cores, topo)
    S = T.sem
    exp = expect[r]
    sent = [0]
    pe, ve = g.tensor, g.vector

    def send(tag):
        src, dests, sem, mask = sends[(r, tag)]
        ids = []
        for d, _b in dests:
            rid, pid, _se = topo.addr(cores[d])
            ids.append((rid, pid))
        if len(dests) == 1:
            g.remote_dma(out_ap=T[dests[0][1]][:], in_ap=T[src][:], remote_sem=S[sem], local_sem=S.sent,
                         pid=ids[0][1], routing_id=ids[0][0], dma_engine_mask=mask)
        else:
            g.remote_dma_fused([RemoteDMATransfer(dst_ids=[DstId(rid=a, pnc=b) for a, b in ids],
                                                  dma_engine_mask=mask, remote_sem=S[sem],
                                                  srcs=[T[src][:]], dsts=[T[b][:] for _d, b in dests])],
                               local_sem=S.sent)
        sent[0] += bin(mask).count("1")

    def has(tag):
        return (r, tag) in sends

    g.sync.dma_start(T.xs[:], T.x[:]).then_inc(S.ld_x, 16)
    g.scalar.dma_start(T.w0[:], T.w[:, 0:256]).then_inc(S.ld_w0, 16)
    g.sync.dma_start(T.w1[:], T.w[:, 256:512]).then_inc(S.ld_w1, 16)
    g.scalar.dma_start(T.w2[:], T.w[:, 512:768]).then_inc(S.ld_w2, 16)
    g.sync.dma_start(T.w3[:], T.w[:, 768:1024]).then_inc(S.ld_w3, 16)

    g.wait_ge(S.ld_x, 16)
    for tag in ("xa", "xr", "xb"):
        if has(tag):
            send(tag)
    if has("w0"):
        g.wait_ge(S.ld_w0, 16)
        send("w0")
    if has("rel"):
        g.wait_ge(S.a_xr, exp["a_xr"])
        send("rel")
    g.wait_ge(S.ld_w2, 16)
    send("w2")
    if has("h1"):
        g.wait_ge(S.act0, 1)
        send("h1")
    g.wait_ge(S.act1, 1)
    send("h2")
    g.wait_ge(S.sent, sent[0])

    def mm(p, w, half, rhs, start, stop):
        return pe.matmul(T[p][:, 0:TK], T[w][:, 128 * half:128 * half + 128], T[rhs][:], start=start, stop=stop)

    pe.wait_ge(S.ld_x, 16)
    pe.wait_ge(S.ld_w0, 16)
    mm("p0", "w0", 0, "xs", True, False)
    if direct[r]:
        pe.wait_ge(S.a_xa, exp["a_xa"])
        mm("p0", "w0", 1, "xa", False, True).then_inc(S.mm0, 1)
    else:
        pe.wait_ge(S.a_xrel, exp["a_xrel"])
        mm("p0", "w0", 1, "xrel", False, True).then_inc(S.mm0, 1)
    pe.wait_ge(S.ld_w1, 16)
    if direct[r ^ 2]:
        pe.wait_ge(S.a_h1, exp["a_h1"])
        mm("p1", "w1", 1, "h1b", True, False)
        pe.wait_ge(S.act0, 1)
        mm("p1", "w1", 0, "h1", False, True).then_inc(S.mm1, 1)
    else:
        pe.wait_ge(S.act0, 1)
        mm("p1", "w1", 0, "h1", True, False)
        pe.wait_ge(S.a_xb, exp["a_xb"])
        pe.wait_ge(S.a_w0, exp["a_w0"])
        mm("p0b", "w0b", 0, "xb", True, False)
        pe.wait_ge(S.a_xrel, exp["a_xrel"])
        mm("p0b", "w0b", 1, "xrel", False, True).then_inc(S.mm0b, 1)
        pe.wait_ge(S.act0b, 1)
        mm("p1", "w1", 1, "h1b", False, True).then_inc(S.mm1, 1)
    pe.wait_ge(S.ld_w2, 16)
    pe.wait_ge(S.act1, 1)
    mm("p2", "w2", 0, "h2", True, False)
    pe.wait_ge(S.a_w2, exp["a_w2"])
    pe.wait_ge(S.a_h2, exp["a_h2"])
    mm("p2", "w2", 1, "h2a", False, True).then_inc(S.mm2, 1)
    mm("p2b", "w2b", 0, "h2b", True, False)
    mm("p2b", "w2b", 1, "h2c", False, True).then_inc(S.mm2b, 1)
    pe.wait_ge(S.ld_w3, 16)
    pe.wait_ge(S.act2, 1)
    mm("p3", "w3", 0, "h3", True, False)
    pe.wait_ge(S.act2b, 1)
    mm("p3", "w3", 1, "h3b", False, True).then_inc(S.mm3, 1)

    ve.memset(T.zero[:], 0.0).then_inc(S.zs, 1)
    ve.wait_ge(S.zs, 1)

    def relu(p, out, k):
        ve.wait_ge(S["mm" + k], 1)
        ve.tensor_tensor(T[out][:], T[p][:, 0:TK], T.zero[:], AluOpType.max).then_inc(S["act" + k], 1)

    relu("p0", "h1", "0")
    if not direct[r ^ 2]:
        relu("p0b", "h1b", "0b")
    relu("p1", "h2", "1")
    relu("p2", "h3", "2")
    relu("p2b", "h3b", "2b")
    relu("p3", "yb", "3")

    g.sync.wait_ge(S.act3, 1)
    g.sync.dma_start(T.y[:], T.yb[:]).then_inc(S.st, 16)
    g.sync.wait_ge(S.st, 16)
